import numpy as np
import ml_dtypes


def mxq(x, axis, fmt="e4m3"):
    dtype, down = {"e4m3": (ml_dtypes.float8_e4m3fn, 7), "e5m2": (ml_dtypes.float8_e5m2, 14)}[fmt]
    v = np.moveaxis(np.asarray(x, np.float32).astype(ml_dtypes.bfloat16).astype(np.float64), axis, -1)
    blocks = v.reshape(v.shape[:-1] + (-1, 32))
    amax = np.abs(blocks).max(-1, keepdims=True)
    byte = np.maximum(np.where(amax > 0, np.frexp(amax)[1] - 1 + 127, 0) - down, 1)
    scale = np.exp2(byte - 127.0)
    codes = (blocks / scale).astype(np.float32).astype(dtype).astype(np.float64)
    return np.moveaxis((codes * scale).reshape(v.shape), -1, axis)


WIDE = False


def mx_kscale(k):
    if not WIDE:
        return np.ones(k)
    levels = np.array([10, -10, 5, -5, 0])
    if k % 512:
        return np.exp2(np.random.permutation(np.resize(levels, k // 32))).repeat(32)
    a = np.empty((k // 512, 16))
    for p in range(k // 512):
        a[p, :8] = np.random.permutation(np.resize(levels, 8))
        for g in range(8):
            far = levels[np.abs(levels - a[p, g]) >= 10]
            a[p, g + 8] = far[np.random.randint(len(far))]
    return np.exp2(a.ravel()).repeat(32)


def f64(x):
    return np.asarray(x).astype(np.float64)


def striped(idx):
    return np.tile(np.asarray(idx).reshape(-1, 16).T, (8, 1)).astype(np.uint16)


def unstriped(offs):
    return offs[:16].T.reshape(-1).astype(np.int64)


E2M1 = np.array([0.0, 0.5, 1.0, 1.5, 2.0, 3.0, 4.0, 6.0, -0.0, -0.5, -1.0, -1.5, -2.0, -3.0, -4.0, -6.0])


def pack_weight(w, fmt):
    k, n = w.shape
    w = f64(np.asarray(w, np.float32).astype(ml_dtypes.bfloat16)).reshape(k // 32, 32, n)
    amax = np.abs(w).max(1)
    if fmt == "e4m3":
        byte = np.frexp(amax)[1] - 1 + 127 - 7
    else:
        mant, ex = np.frexp(amax / 6.0)
        byte = np.where(mant > 0.5, ex, ex - 1) + 127
    byte = np.clip(np.where(amax > 0, byte, 1), 1, 254)
    scaled = (w * np.exp2(127.0 - byte)[:, None, :]).reshape(k, n).astype(np.float32)
    by_word = np.ascontiguousarray(scaled.reshape(k // 512, 128, 4, n).transpose(0, 1, 3, 2))
    if fmt == "e4m3":
        words = by_word.astype(ml_dtypes.float8_e4m3fn).view(np.uint8)
    else:
        c = by_word.astype(ml_dtypes.float4_e2m1fn).view(np.uint8) & 0xF
        words = (c[..., 0::2] | (c[..., 1::2] << 4)).reshape(k // 512, 128, 2 * n)
    return np.ascontiguousarray(words), np.ascontiguousarray(byte.astype(np.uint8).reshape(k // 512, 16, n))


def unpack_weight(words, scales, fmt):
    g, _, n = scales.shape
    words = np.ascontiguousarray(words).reshape(g, 128, n, -1)
    if fmt == "e4m3":
        vals = words.view(ml_dtypes.float8_e4m3fn).astype(np.float64)
    else:
        nib = np.empty((g, 128, n, 4), np.uint8)
        nib[..., 0::2] = words & 0xF
        nib[..., 1::2] = words >> 4
        vals = E2M1[nib]
    vals = vals * np.repeat(np.exp2(scales.astype(np.float64) - 127.0), 8, axis=1)[..., None]
    return vals.transpose(0, 1, 3, 2).reshape(g * 512, n)


K, T, J, I = 512, 2048, 512, 512


def setup_inputs():
    n = np.random.standard_normal
    idx = np.random.permutation(T)[:J]
    fj = mx_kscale(J)
    knp = pack_weight(n((J, I)) * 1 / np.sqrt(J) * fj[:, None], "e4m3")
    return {
        "xf": (n((K, T))).astype(np.float32),
        "rw": (np.random.uniform(0.5, 2.0, (1, J)) / fj).astype(np.float32),
        "kn_words": knp[0],
        "kn_scales": knp[1],
        "old": (1.0 * n((K, I))).astype(np.float32),
        "offs": striped(idx),
    }


def reference(xf, rw, kn_words, kn_scales, old, offs):
    idx = unstriped(offs)
    knu = unpack_weight(kn_words, kn_scales, "e4m3")
    xs = f64(xf)[:, idx] * f64(rw)
    xj = xs.T
    xjq = mxq(xj, 0, "e4m3")
    f1 = xjq.T @ knu
    y = f1 + 0.5 * f64(old)
    return y

@@ -1,0 +1,126 @@
+from contextlib import ExitStack
+
+import concourse.mybir as mybir
+from concourse.masks import make_identity
+
+K, T, J, I = 512, 2048, 512, 512
+FLOPS = 2 * K * J * I
+
+F32 = mybir.dt.float32
+BF16 = mybir.dt.bfloat16
+I32 = mybir.dt.int32
+U32 = mybir.dt.uint32
+U16 = mybir.dt.uint16
+U8 = mybir.dt.uint8
+FP8X4 = mybir.dt.float8_e4m3fn_x4
+MULT = mybir.AluOpType.mult
+ADD = mybir.AluOpType.add
+
+P = 128
+PACK = 4
+NB = K // P
+HALF = J // 2
+
+
+def tile_list_slots_to_knots_kernel(tc, xf, rw, kn_words, kn_scales, old, offs, out):
+    nc = tc.nc
+    xf_b = xf.rearrange("(p b) t -> p b t", b=NB)
+    old_b = old.rearrange("(p b) i -> p b i", b=NB)
+    out_b = out.rearrange("(p b) i -> p b i", b=NB)
+
+    with ExitStack() as ctx:
+        keep = ctx.enter_context(tc.tile_pool(name="keep", bufs=1))
+        ring = ctx.enter_context(tc.tile_pool(name="ring", bufs=2))
+        psum = ctx.enter_context(tc.psum_pool(name="psum", bufs=1))
+
+        offsets = keep.tile([P, J // 16], U16, name="offsets")
+        tokens = [keep.tile([P, T], F32, name="tokens%d" % b, tag="slot%d" % b, align_bytes=64) for b in range(NB)]
+        rw_cols = keep.tile([P, PACK], F32, name="rw_cols")
+        kn_codes = keep.tile([P, I], U32, name="kn_codes", align_bytes=64)
+        kn_plane = keep.tile([P, I], U8, name="kn_plane", align_bytes=64)
+        olds = [keep.tile([P, n, I], F32, name="old%d" % h, tag="oldslot%d" % h, align_bytes=64) for h, n in enumerate((1, 1, 1, 1))]
+        ident = keep.tile([P, P], F32, name="ident")
+        rw_rows = keep.tile([P, J], F32, name="rw_rows")
+
+        nc.sync.dma_start(out=rw_cols[:], in_=rw.rearrange("o (p t) -> (o p) t", t=PACK))
+        nc.sync.dma_start(out=tokens[0][:], in_=xf_b[:, 0, :])
+        nc.sync.dma_start(offsets[:], offs)
+        for q in range(4):
+            nc.sync.dma_start(out=kn_plane[32 * q : 32 * q + 4, :].bitcast(I32), in_=kn_scales[0, 4 * q : 4 * q + 4, :].bitcast(I32))
+        for b in range(1, NB):
+            nc.sync.dma_start(out=tokens[b][:], in_=xf_b[:, b, :])
+        nc.sync.dma_start(out=kn_codes[:].bitcast(I32), in_=kn_words[0].rearrange("p n t -> p (n t)").bitcast(I32))
+        for h, n in enumerate((1, 1, 1, 1)):
+            nc.sync.dma_start(out=olds[h][:], in_=old_b[:, h : h + n, :])
+
+        make_identity(nc, ident[:])
+
+        spread = psum.tile([P, PACK, P], F32, name="spread", tag="turn1")
+        for t in range(PACK):
+            nc.tensor.transpose(spread[:, t, :], rw_cols[:, t : t + 1].to_broadcast([P, P]), ident[:])
+        nc.scalar.copy(out=rw_rows[:].rearrange("m (n t) -> m n t", t=PACK), in_=spread[:].rearrange("m t n -> m n t"))
+
+        grouped = {}
+        codes = {}
+        planes = {}
+
+        def pick(b):
+            rounded = ring.tile([P, J], BF16, name="rounded", align_bytes=64)
+            for h in range(2):
+                cols = slice(h * HALF, (h + 1) * HALF)
+                picked = ring.tile([P, HALF], F32, name="picked%d" % h)
+                nc.vector.tensor_tensor(picked[:], tokens[b][:].indirect(offsets[:, h * 16 : (h + 1) * 16]), rw_rows[:, cols], MULT)
+                nc.scalar.copy(out=rounded[:, cols], in_=picked[:])
+            words = rounded[:].bitcast(F32)
+            turned = psum.tile([P, 2, P], F32, name="turned", tag="turn%d" % (b % 2))
+            for u in range(2):
+                nc.tensor.transpose(turned[:, u, :], words[:, u : 2 * P : 2], ident[:])
+            grouped[b] = keep.tile([P, P * PACK], BF16, name="grouped%d" % b, tag="grouped%d_0" % b, align_bytes=64)
+            nc.scalar.copy(out=grouped[b][:].bitcast(F32).rearrange("p (r u) -> p r u", u=2), in_=turned[:].rearrange("p u r -> p r u"))
+
+        def quantise(b, tag):
+            codes[b] = keep.tile([P, P], U32, name="codes%d" % b, tag=tag, align_bytes=64)
+            planes[b] = keep.tile([P, P], U8, name="plane%d" % b, align_bytes=64)
+            nc.vector.quantize_mx(out=codes[b][:].bitcast(FP8X4), scales=planes[b][:], in_=grouped[b][:])
+
+        accs = {}
+
+        def multiply(b, parts):
+            width = I // parts
+            for s in range(parts):
+                cols = slice(s * width, (s + 1) * width)
+                accs[b, s] = psum.tile([P, width], F32, name="acc", tag="acc%d_%d" % (b, s))
+                nc.tensor.matmul_mx(
+                    out=accs[b, s][:],
+                    lhsT=codes[b][:].bitcast(FP8X4),
+                    lhsT_scale=planes[b][:],
+                    rhs=kn_codes[:, cols].bitcast(FP8X4),
+                    rhs_scale=kn_plane[:, cols],
+                    start=True,
+                    stop=True,
+                )
+
+        def finish(b, parts, tag):
+            width = I // parts
+            for s in range(parts):
+                cols = slice(s * width, (s + 1) * width)
+                res = keep.tile([P, width], F32, name="res%d_%d" % (b, s), tag=tag[s], align_bytes=64)
+                nc.vector.scalar_tensor_tensor(res[:], olds[b][:, 0, cols], 0.5, accs[b, s][:], MULT, ADD)
+                nc.sync.dma_start(out=out_b[:, b, cols], in_=res[:])
+
+        pick(0)
+        pick(1)
+        quantise(0, "slot1")
+        pick(2)
+        quantise(1, "slot2")
+        multiply(0, 1)
+        multiply(1, 1)
+        pick(3)
+        finish(0, 1, ["res0"])
+        quantise(2, "oldslot0")
+        multiply(2, 1)
+        finish(1, 1, ["res1"])
+        quantise(3, "oldslot1")
+        finish(2, 1, ["grouped3_0"])
+        multiply(3, 2)
+        finish(3, 2, ["oldslot2", "res3"])

@@ -18,43 +18,59 @@ ADD = mybir.AluOpType.add
 
 P = 128
 PACK = 4
-NB = K // P
-HALF = J // 2
+BLOCKS = K // P
+QUADRANT = 32
+PER_COLUMN = 16
+
+GATHER_PIECES = ((0, 352), (352, J))
+
+WHOLE = ((0, I),)
+HALVES = ((0, I // 2), (I // 2, I))
+
+CODES_BYTES = 4 * P
 
 
 def tile_list_slots_to_knots_kernel(tc, xf, rw, kn_words, kn_scales, old, offs, out):
     nc = tc.nc
-    xf_b = xf.rearrange("(p b) t -> p b t", b=NB)
-    old_b = old.rearrange("(p b) i -> p b i", b=NB)
-    out_b = out.rearrange("(p b) i -> p b i", b=NB)
+    xf_blocks = xf.rearrange("(m b) t -> m b t", b=BLOCKS)
+    old_blocks = old.rearrange("(m b) i -> m b i", b=BLOCKS)
+    out_blocks = out.rearrange("(m b) i -> m b i", b=BLOCKS)
 
     with ExitStack() as ctx:
         keep = ctx.enter_context(tc.tile_pool(name="keep", bufs=1))
         ring = ctx.enter_context(tc.tile_pool(name="ring", bufs=2))
+        placed = ctx.enter_context(tc.tile_pool(name="placed", bufs=1))
         psum = ctx.enter_context(tc.psum_pool(name="psum", bufs=1))
 
-        offsets = keep.tile([P, J // 16], U16, name="offsets")
-        tokens = [keep.tile([P, T], F32, name="tokens%d" % b, tag="slot%d" % b, align_bytes=64) for b in range(NB)]
+        offsets = keep.tile([P, J // PER_COLUMN], U16, name="offsets")
+        tokens = [keep.tile([P, T], F32, name="tokens", tag="tokens%d" % b, align_bytes=64) for b in range(BLOCKS)]
         rw_cols = keep.tile([P, PACK], F32, name="rw_cols")
+        rw_rows = keep.tile([P, J], F32, name="rw_rows")
         kn_codes = keep.tile([P, I], U32, name="kn_codes", align_bytes=64)
         kn_plane = keep.tile([P, I], U8, name="kn_plane", align_bytes=64)
-        olds = [keep.tile([P, n, I], F32, name="old%d" % h, tag="oldslot%d" % h, align_bytes=64) for h, n in enumerate((1, 1, 1, 1))]
         ident = keep.tile([P, P], F32, name="ident")
-        rw_rows = keep.tile([P, J], F32, name="rw_rows")
+        olds = [placed.tile([P, I], F32, name="old0", offset=0, align_bytes=64)]
+        olds.extend(keep.tile([P, I], F32, name="old%d" % b) for b in range(1, BLOCKS))
 
+        def load_scale_rows(q):
+            rows = kn_scales[0, PACK * q : PACK * (q + 1), :]
+            nc.sync.dma_start(out=kn_plane[QUADRANT * q : QUADRANT * q + PACK, :].bitcast(I32), in_=rows.bitcast(I32))
+
+        nc.scalar.dma_start(out=tokens[0][:, : T // 2], in_=xf_blocks[:, 0, : T // 2])
         nc.sync.dma_start(out=rw_cols[:], in_=rw.rearrange("o (p t) -> (o p) t", t=PACK))
-        nc.sync.dma_start(out=tokens[0][:], in_=xf_b[:, 0, :])
         nc.sync.dma_start(offsets[:], offs)
-        for q in range(4):
-            nc.sync.dma_start(out=kn_plane[32 * q : 32 * q + 4, :].bitcast(I32), in_=kn_scales[0, 4 * q : 4 * q + 4, :].bitcast(I32))
-        for b in range(1, NB):
-            nc.sync.dma_start(out=tokens[b][:], in_=xf_b[:, b, :])
+        for q in range(3):
+            load_scale_rows(q)
+        nc.sync.dma_start(out=tokens[0][:, T // 2 :], in_=xf_blocks[:, 0, T // 2 :])
+        nc.sync.dma_start(out=tokens[1][:], in_=xf_blocks[:, 1, :])
+        load_scale_rows(3)
+        for b in range(2, BLOCKS):
+            nc.sync.dma_start(out=tokens[b][:], in_=xf_blocks[:, b, :])
         nc.sync.dma_start(out=kn_codes[:].bitcast(I32), in_=kn_words[0].rearrange("p n t -> p (n t)").bitcast(I32))
-        for h, n in enumerate((1, 1, 1, 1)):
-            nc.sync.dma_start(out=olds[h][:], in_=old_b[:, h : h + n, :])
+        for b in range(BLOCKS):
+            nc.sync.dma_start(out=olds[b][:], in_=old_blocks[:, b, :])
 
         make_identity(nc, ident[:])
-
         spread = psum.tile([P, PACK, P], F32, name="spread", tag="turn1")
         for t in range(PACK):
             nc.tensor.transpose(spread[:, t, :], rw_cols[:, t : t + 1].to_broadcast([P, P]), ident[:])
@@ -63,64 +79,61 @@ def tile_list_slots_to_knots_kernel(tc, xf, rw, kn_words, kn_scales, old, offs, 
         grouped = {}
         codes = {}
         planes = {}
+        sums = {}
 
         def pick(b):
             rounded = ring.tile([P, J], BF16, name="rounded", align_bytes=64)
-            for h in range(2):
-                cols = slice(h * HALF, (h + 1) * HALF)
-                picked = ring.tile([P, HALF], F32, name="picked%d" % h)
-                nc.vector.tensor_tensor(picked[:], tokens[b][:].indirect(offsets[:, h * 16 : (h + 1) * 16]), rw_rows[:, cols], MULT)
-                nc.scalar.copy(out=rounded[:, cols], in_=picked[:])
-            words = rounded[:].bitcast(F32)
+            for j0, j1 in GATHER_PIECES:
+                picked = ring.tile([P, j1 - j0], F32, name="picked%d" % j0)
+                window = tokens[b][:].indirect(offsets[:, j0 // PER_COLUMN : j1 // PER_COLUMN])
+                nc.vector.tensor_tensor(picked[:], window, rw_rows[:, j0:j1], MULT)
+                nc.scalar.copy(out=rounded[:, j0:j1], in_=picked[:])
+            pairs = rounded[:].bitcast(F32)
             turned = psum.tile([P, 2, P], F32, name="turned", tag="turn%d" % (b % 2))
             for u in range(2):
-                nc.tensor.transpose(turned[:, u, :], words[:, u : 2 * P : 2], ident[:])
-            grouped[b] = keep.tile([P, P * PACK], BF16, name="grouped%d" % b, tag="grouped%d_0" % b, align_bytes=64)
-            nc.scalar.copy(out=grouped[b][:].bitcast(F32).rearrange("p (r u) -> p r u", u=2), in_=turned[:].rearrange("p u r -> p r u"))
+                nc.tensor.transpose(turned[:, u, :], pairs[:, u : 2 * P : 2], ident[:])
+            grouped[b] = keep.tile([P, P * PACK], BF16, name="grouped%d" % b, align_bytes=64)
+            nc.scalar.copy(
+                out=grouped[b][:].bitcast(F32).rearrange("p (m u) -> p m u", u=2),
+                in_=turned[:].rearrange("p u m -> p m u"),
+            )
 
-        def quantise(b, tag):
-            codes[b] = keep.tile([P, P], U32, name="codes%d" % b, tag=tag, align_bytes=64)
+        def quantise(b, codes_tile):
+            codes[b] = codes_tile
             planes[b] = keep.tile([P, P], U8, name="plane%d" % b, align_bytes=64)
             nc.vector.quantize_mx(out=codes[b][:].bitcast(FP8X4), scales=planes[b][:], in_=grouped[b][:])
 
-        accs = {}
-
-        def multiply(b, parts):
-            width = I // parts
-            for s in range(parts):
-                cols = slice(s * width, (s + 1) * width)
-                accs[b, s] = psum.tile([P, width], F32, name="acc", tag="acc%d_%d" % (b, s))
+        def multiply(b, ranges):
+            for i0, i1 in ranges:
+                sums[b, i0] = psum.tile([P, i1 - i0], F32, name="sums%d_%d" % (b, i0))
                 nc.tensor.matmul_mx(
-                    out=accs[b, s][:],
+                    out=sums[b, i0][:],
                     lhsT=codes[b][:].bitcast(FP8X4),
                     lhsT_scale=planes[b][:],
-                    rhs=kn_codes[:, cols].bitcast(FP8X4),
-                    rhs_scale=kn_plane[:, cols],
+                    rhs=kn_codes[:, i0:i1].bitcast(FP8X4),
+                    rhs_scale=kn_plane[:, i0:i1],
                     start=True,
                     stop=True,
                 )
 
-        def finish(b, parts, tag):
-            width = I // parts
-            for s in range(parts):
-                cols = slice(s * width, (s + 1) * width)
-                res = keep.tile([P, width], F32, name="res%d_%d" % (b, s), tag=tag[s], align_bytes=64)
-                nc.vector.scalar_tensor_tensor(res[:], olds[b][:, 0, cols], 0.5, accs[b, s][:], MULT, ADD)
-                nc.sync.dma_start(out=out_b[:, b, cols], in_=res[:])
+        def add_and_store(b, ranges, result):
+            for i0, i1 in ranges:
+                nc.vector.scalar_tensor_tensor(result[:, i0:i1], olds[b][:, i0:i1], 0.5, sums[b, i0][:], MULT, ADD)
+                nc.sync.dma_start(out=out_blocks[:, b, i0:i1], in_=result[:, i0:i1])
 
         pick(0)
-        pick(1)
-        quantise(0, "slot1")
-        pick(2)
-        quantise(1, "slot2")
-        multiply(0, 1)
-        multiply(1, 1)
+        for b in range(2):
+            pick(b + 1)
+            quantise(b, keep.tile([P, P], U32, name="codes", tag="tokens%d" % (b + 1), align_bytes=64))
+        for b in range(2):
+            multiply(b, WHOLE)
         pick(3)
-        finish(0, 1, ["res0"])
-        quantise(2, "oldslot0")
-        multiply(2, 1)
-        finish(1, 1, ["res1"])
-        quantise(3, "oldslot1")
-        finish(2, 1, ["grouped3_0"])
-        multiply(3, 2)
-        finish(3, 2, ["oldslot2", "res3"])
+
+        add_and_store(0, WHOLE, keep.tile([P, I], F32, name="result0"))
+        quantise(2, placed.tile([P, P], U32, name="codes2", offset=0, align_bytes=64))
+        multiply(2, HALVES)
+        add_and_store(1, WHOLE, placed.tile([P, I], F32, name="result1", offset=CODES_BYTES, align_bytes=64))
+        quantise(3, keep.tile([P, P], U32, name="codes3", align_bytes=64))
+        add_and_store(2, HALVES, keep.tile([P, I], F32, name="result2"))
+        multiply(3, HALVES)
+        add_and_store(3, HALVES, keep.tile([P, I], F32, name="result3"))

@@ -23,6 +23,7 @@ QUADRANT = 32
 PER_COLUMN = 16
 
 GATHER_PIECES = ((0, 352), (352, J))
+WHOLE_LIST = ((0, J),)
 
 WHOLE = ((0, I),)
 HALVES = ((0, I // 2), (I // 2, I))
@@ -49,8 +50,9 @@ def tile_list_slots_to_knots_kernel(tc, xf, rw, kn_words, kn_scales, old, offs, 
         kn_codes = keep.tile([P, I], U32, name="kn_codes", align_bytes=64)
         kn_plane = keep.tile([P, I], U8, name="kn_plane", align_bytes=64)
         ident = keep.tile([P, P], F32, name="ident")
-        olds = [placed.tile([P, I], F32, name="old0", offset=0, align_bytes=64)]
-        olds.extend(keep.tile([P, I], F32, name="old%d" % b) for b in range(1, BLOCKS))
+        old0 = placed.tile([P, I], F32, name="old0", offset=0, align_bytes=64)
+        old1 = keep.tile([P, I], F32, name="old1")
+        old23 = keep.tile([P, 2, I], F32, name="old23")
 
         def load_scale_rows(q):
             rows = kn_scales[0, PACK * q : PACK * (q + 1), :]
@@ -67,8 +69,10 @@ def tile_list_slots_to_knots_kernel(tc, xf, rw, kn_words, kn_scales, old, offs, 
         for b in range(2, BLOCKS):
             nc.sync.dma_start(out=tokens[b][:], in_=xf_blocks[:, b, :])
         nc.sync.dma_start(out=kn_codes[:].bitcast(I32), in_=kn_words[0].rearrange("p n t -> p (n t)").bitcast(I32))
-        for b in range(BLOCKS):
-            nc.sync.dma_start(out=olds[b][:], in_=old_blocks[:, b, :])
+        nc.sync.dma_start(out=old0[:], in_=old_blocks[:, 0, :])
+        nc.sync.dma_start(out=old1[:], in_=old_blocks[:, 1, :])
+        nc.sync.dma_start(out=old23[:], in_=old_blocks[:, 2:4, :])
+        olds = [old0[:], old1[:], old23[:, 0, :], old23[:, 1, :]]
 
         make_identity(nc, ident[:])
         spread = psum.tile([P, PACK, P], F32, name="spread", tag="turn1")
@@ -81,9 +85,9 @@ def tile_list_slots_to_knots_kernel(tc, xf, rw, kn_words, kn_scales, old, offs, 
         planes = {}
         sums = {}
 
-        def pick(b):
+        def pick(b, pieces):
             rounded = ring.tile([P, J], BF16, name="rounded", align_bytes=64)
-            for j0, j1 in GATHER_PIECES:
+            for j0, j1 in pieces:
                 picked = ring.tile([P, j1 - j0], F32, name="picked%d" % j0)
                 window = tokens[b][:].indirect(offsets[:, j0 // PER_COLUMN : j1 // PER_COLUMN])
                 nc.vector.tensor_tensor(picked[:], window, rw_rows[:, j0:j1], MULT)
@@ -121,13 +125,13 @@ def tile_list_slots_to_knots_kernel(tc, xf, rw, kn_words, kn_scales, old, offs, 
                 nc.vector.scalar_tensor_tensor(result[:, i0:i1], olds[b][:, i0:i1], 0.5, sums[b, i0][:], MULT, ADD)
                 nc.sync.dma_start(out=out_blocks[:, b, i0:i1], in_=result[:, i0:i1])
 
-        pick(0)
+        pick(0, WHOLE_LIST)
         for b in range(2):
-            pick(b + 1)
+            pick(b + 1, WHOLE_LIST)
             quantise(b, keep.tile([P, P], U32, name="codes", tag="tokens%d" % (b + 1), align_bytes=64))
         for b in range(2):
             multiply(b, WHOLE)
-        pick(3)
+        pick(3, GATHER_PIECES)
 
         add_and_store(0, WHOLE, keep.tile([P, I], F32, name="result0"))
         quantise(2, placed.tile([P, P], U32, name="codes2", offset=0, align_bytes=64))

from contextlib import ExitStack

import concourse.mybir as mybir
from concourse.masks import make_identity

K, T, J, I = 512, 2048, 512, 512
FLOPS = 2 * K * J * I

F32 = mybir.dt.float32
BF16 = mybir.dt.bfloat16
I32 = mybir.dt.int32
U32 = mybir.dt.uint32
U16 = mybir.dt.uint16
U8 = mybir.dt.uint8
FP8X4 = mybir.dt.float8_e4m3fn_x4
MULT = mybir.AluOpType.mult
ADD = mybir.AluOpType.add

P = 128
PACK = 4
BLOCKS = K // P
QUADRANT = 32
PER_COLUMN = 16

GATHER_PIECES = ((0, 352), (352, J))
WHOLE_LIST = ((0, J),)

WHOLE = ((0, I),)
HALVES = ((0, I // 2), (I // 2, I))

CODES_BYTES = 4 * P


def tile_list_slots_to_knots_kernel(tc, xf, rw, kn_words, kn_scales, old, offs, out):
    nc = tc.nc
    xf_blocks = xf.rearrange("(m b) t -> m b t", b=BLOCKS)
    old_blocks = old.rearrange("(m b) i -> m b i", b=BLOCKS)
    out_blocks = out.rearrange("(m b) i -> m b i", b=BLOCKS)

    with ExitStack() as ctx:
        keep = ctx.enter_context(tc.tile_pool(name="keep", bufs=1))
        ring = ctx.enter_context(tc.tile_pool(name="ring", bufs=2))
        placed = ctx.enter_context(tc.tile_pool(name="placed", bufs=1))
        psum = ctx.enter_context(tc.psum_pool(name="psum", bufs=1))

        offsets = keep.tile([P, J // PER_COLUMN], U16, name="offsets")
        tokens = [keep.tile([P, T], F32, name="tokens", tag="tokens%d" % b, align_bytes=64) for b in range(BLOCKS)]
        rw_cols = keep.tile([P, PACK], F32, name="rw_cols")
        rw_rows = keep.tile([P, J], F32, name="rw_rows")
        kn_codes = keep.tile([P, I], U32, name="kn_codes", align_bytes=64)
        kn_plane = keep.tile([P, I], U8, name="kn_plane", align_bytes=64)
        ident = keep.tile([P, P], F32, name="ident")
        old0 = placed.tile([P, I], F32, name="old0", offset=0, align_bytes=64)
        old1 = keep.tile([P, I], F32, name="old1")
        old23 = keep.tile([P, 2, I], F32, name="old23")

        def load_scale_rows(q):
            rows = kn_scales[0, PACK * q : PACK * (q + 1), :]
            nc.sync.dma_start(out=kn_plane[QUADRANT * q : QUADRANT * q + PACK, :].bitcast(I32), in_=rows.bitcast(I32))

        nc.scalar.dma_start(out=tokens[0][:, : T // 2], in_=xf_blocks[:, 0, : T // 2])
        nc.sync.dma_start(out=rw_cols[:], in_=rw.rearrange("o (p t) -> (o p) t", t=PACK))
        nc.sync.dma_start(offsets[:], offs)
        for q in range(3):
            load_scale_rows(q)
        nc.sync.dma_start(out=tokens[0][:, T // 2 :], in_=xf_blocks[:, 0, T // 2 :])
        nc.sync.dma_start(out=tokens[1][:], in_=xf_blocks[:, 1, :])
        load_scale_rows(3)
        for b in range(2, BLOCKS):
            nc.sync.dma_start(out=tokens[b][:], in_=xf_blocks[:, b, :])
        nc.sync.dma_start(out=kn_codes[:].bitcast(I32), in_=kn_words[0].rearrange("p n t -> p (n t)").bitcast(I32))
        nc.sync.dma_start(out=old0[:], in_=old_blocks[:, 0, :])
        nc.sync.dma_start(out=old1[:], in_=old_blocks[:, 1, :])
        nc.sync.dma_start(out=old23[:], in_=old_blocks[:, 2:4, :])
        olds = [old0[:], old1[:], old23[:, 0, :], old23[:, 1, :]]

        make_identity(nc, ident[:])
        spread = psum.tile([P, PACK, P], F32, name="spread", tag="turn1")
        for t in range(PACK):
            nc.tensor.transpose(spread[:, t, :], rw_cols[:, t : t + 1].to_broadcast([P, P]), ident[:])
        nc.scalar.copy(out=rw_rows[:].rearrange("m (n t) -> m n t", t=PACK), in_=spread[:].rearrange("m t n -> m n t"))

        grouped = {}
        codes = {}
        planes = {}
        sums = {}

        def pick(b, pieces):
            rounded = ring.tile([P, J], BF16, name="rounded", align_bytes=64)
            for j0, j1 in pieces:
                picked = ring.tile([P, j1 - j0], F32, name="picked%d" % j0)
                window = tokens[b][:].indirect(offsets[:, j0 // PER_COLUMN : j1 // PER_COLUMN])
                nc.vector.tensor_tensor(picked[:], window, rw_rows[:, j0:j1], MULT)
                nc.scalar.copy(out=rounded[:, j0:j1], in_=picked[:])
            pairs = rounded[:].bitcast(F32)
            turned = psum.tile([P, 2, P], F32, name="turned", tag="turn%d" % (b % 2))
            for u in range(2):
                nc.tensor.transpose(turned[:, u, :], pairs[:, u : 2 * P : 2], ident[:])
            grouped[b] = keep.tile([P, P * PACK], BF16, name="grouped%d" % b, align_bytes=64)
            nc.scalar.copy(
                out=grouped[b][:].bitcast(F32).rearrange("p (m u) -> p m u", u=2),
                in_=turned[:].rearrange("p u m -> p m u"),
            )

        def quantise(b, codes_tile):
            codes[b] = codes_tile
            planes[b] = keep.tile([P, P], U8, name="plane%d" % b, align_bytes=64)
            nc.vector.quantize_mx(out=codes[b][:].bitcast(FP8X4), scales=planes[b][:], in_=grouped[b][:])

        def multiply(b, ranges):
            for i0, i1 in ranges:
                sums[b, i0] = psum.tile([P, i1 - i0], F32, name="sums%d_%d" % (b, i0))
                nc.tensor.matmul_mx(
                    out=sums[b, i0][:],
                    lhsT=codes[b][:].bitcast(FP8X4),
                    lhsT_scale=planes[b][:],
                    rhs=kn_codes[:, i0:i1].bitcast(FP8X4),
                    rhs_scale=kn_plane[:, i0:i1],
                    start=True,
                    stop=True,
                )

        def add_and_store(b, ranges, result):
            for i0, i1 in ranges:
                nc.vector.scalar_tensor_tensor(result[:, i0:i1], olds[b][:, i0:i1], 0.5, sums[b, i0][:], MULT, ADD)
                nc.sync.dma_start(out=out_blocks[:, b, i0:i1], in_=result[:, i0:i1])

        pick(0, WHOLE_LIST)
        for b in range(2):
            pick(b + 1, WHOLE_LIST)
            quantise(b, keep.tile([P, P], U32, name="codes", tag="tokens%d" % (b + 1), align_bytes=64))
        for b in range(2):
            multiply(b, WHOLE)
        pick(3, GATHER_PIECES)

        add_and_store(0, WHOLE, keep.tile([P, I], F32, name="result0"))
        quantise(2, placed.tile([P, P], U32, name="codes2", offset=0, align_bytes=64))
        multiply(2, HALVES)
        add_and_store(1, WHOLE, placed.tile([P, I], F32, name="result1", offset=CODES_BYTES, align_bytes=64))
        quantise(3, keep.tile([P, P], U32, name="codes3", align_bytes=64))
        add_and_store(2, HALVES, keep.tile([P, I], F32, name="result2"))
        multiply(3, HALVES)
        add_and_store(3, HALVES, keep.tile([P, I], F32, name="result3"))
